import numpy as np, ml_dtypes
CORES = [9,25,41,57]
N = 4
BF = ml_dtypes.bfloat16
def gentries(a):
    return np.ascontiguousarray(a.reshape(8, 16, -1).transpose(0, 2, 1)).reshape(8, -1)
def gtable(e):
    e = np.asarray(e); return np.ascontiguousarray(e.reshape(8, -1, 16).transpose(0, 2, 1)).reshape(128, -1).astype(np.int32)
def f(rng, *shape):
    return (rng.standard_normal(shape, dtype=np.float32) * np.exp2(rng.integers(-2, 3, shape[:-1] + (1,)))).astype(BF)
def wide(rng, *shape):
    v = f(rng, *shape).astype(np.float32); k = shape[:-2] + (1, shape[-1])
    return (v * np.exp2(rng.integers(-6, 7, k)) * (rng.random(k) > 0.0625)).astype(BF)
V, G, E, C, M, H = 2048, 256, 6, 4, 560, 80
ORDER = [0, 1, 2, 3, 0, 1, 2, 3]
W = V + (N - 1) * G
def ghosts(z, S):
    for r in range(N):
        for d in range(N - 1):
            s = (r + 1 + d) % N
            z[r, :, :, V + d * G:V + (d + 1) * G] = np.take_along_axis(z[s, :, :, :V], S[s][:, N - 2 - d][:, None, :], 2)
def halos(halo):
    return np.stack([gentries(v) for v in halo]).reshape(N, 8, N - 1, G).astype(np.int64)
def around(hue, S):
    w = np.zeros((N, 8, 1, W), np.int64); w[:, :, 0, :V] = hue; ghosts(w, S); return w[:, :, 0]
def counts(rng, n, cap, fill):
    if rng.random() < fill: return rng.permutation(np.minimum(np.maximum(n - cap * np.arange(C), 0), cap))
    return np.bincount(rng.permutation(np.repeat(np.arange(C), cap))[:n], minlength=C)
def single(rng, v):
    return v.astype(np.float32) * (rng.random(v.shape, dtype=np.float32) + np.float32(0.5))
def make(rng, fill, rep, lo):
    hue = np.zeros((N, 8, V), np.int32); S = np.zeros((N, 8, N - 1, G), np.int64); nb = np.zeros((N, 8, E, V), np.int32)
    for r in range(N):
        for g in range(8):
            n = counts(rng, V, M, fill); o = rng.permutation(C); h = np.repeat(o, n[o])
            if not rep: h = rng.permutation(h)
            hue[r, g] = h; own = [np.flatnonzero(h == c) for c in range(C)]
            for d in range(N - 1):
                n = counts(rng, G, H, fill)
                S[r, g, d] = rng.permutation(np.concatenate([own[c][-rng.integers(0, 2, n[c])] if rep else rng.permutation(own[c])[:n[c]] for c in range(C)]))
    w = around(hue, S)
    for r in range(N):
        for g in range(8):
            k = w[r, g, lo:]; o = np.argsort(k, kind="stable"); n = np.bincount(k, minlength=C); a = np.add.accumulate(n) - n; c = hue[r, g]
            u = rng.integers(0, (len(k) - n[c])[None, :], (E, V)); u = u + n[c] * (u >= a[c]); p = lo + o[u]
            if rep:
                p[3:] = p[2]; p[0] = np.where(c != w[r, g, 0], 0, p[0]); p[1] = np.where(c != w[r, g, W - 1], W - 1, p[1])
            nb[r, g] = p
    co = (rng.random((N, 8, E * V)) - 0.5) * 0.5
    if rep: co = co * (rng.random(co.shape) > 0.25)
    return {"x": single(rng, f(rng, N, 128, V)), "b": f(rng, N, 128, V), "nb": nb.reshape(N, 8, E * V), "co": co.astype(np.float32).astype(BF), "di": (0.5 + 0.5 * rng.random((N, 8, V))).astype(np.float32),
            "hue": hue, "halo": np.stack([gtable(S[r].reshape(8, -1)) for r in range(N)])}
def setup_inputs(rng):
    return make(rng, 0.25, False, 0)
def setup_inputs_full(rng):
    return make(rng, 2.0, False, 0)
def setup_inputs_repeats(rng):
    return make(rng, 0.5, True, 0)
def setup_inputs_ghosts(rng):
    return make(rng, 0.25, False, V)
def setup_inputs_spread(rng):
    d = make(rng, 0.25, False, 0); d["x"] = single(rng, wide(rng, N, 128, V)); d["b"] = wide(rng, N, 128, V); return d
def check_inputs(d):
    bad = []; hue, nb, S = d["hue"], d["nb"], halos(d["halo"])
    if hue.min() < 0 or hue.max() >= C: bad.append("colours")
    if S.min() < 0 or S.max() >= V: bad.append("halo")
    if nb.min() < 0 or nb.max() >= W: bad.append("places")
    if not (np.abs(d["x"]) <= 2.0 ** 30).all() or not (np.abs(d["b"].astype(np.float32)) <= 2.0 ** 30).all(): bad.append("sizes")
    if not (np.abs(d["co"].astype(np.float32)) <= 0.5).all(): bad.append("coefficients")
    if not ((d["di"] > 0) & (d["di"] <= 1)).all(): bad.append("diagonals")
    if bad: return bad
    w = around(hue, S); q = w[:, :, V:].reshape(N, 8, N - 1, G)
    if max(np.count_nonzero(hue == c, axis=2).max() for c in range(C)) > M: bad.append("vertices of a colour")
    if max(np.count_nonzero(q == c, axis=3).max() for c in range(C)) > H: bad.append("halo entries of a colour")
    if (np.take_along_axis(w, nb.astype(np.int64), 2).reshape(N, 8, E, V) == hue[:, :, None]).any(): bad.append("neighbours")
    return bad
def reference(x, b, nb, co, di, hue, halo):
    S = halos(halo); P = nb.reshape(N, 8, E, V); A = co.astype(np.float64).reshape(N, 8, E, V); D = di.astype(np.float64); R = b.astype(np.float64).reshape(N, 8, 16, V)
    z = np.zeros((N, 8, 16, W), np.float64); z[..., :V] = x.reshape(N, 8, 16, V); ghosts(z, S)
    for c in ORDER:
        for r in range(N):
            for g in range(8):
                v = np.flatnonzero(hue[r, g] == c); s = np.zeros((16, len(v)), np.float64)
                for e in range(E): s += A[r, g, e, v] * z[r, g][:, P[r, g, e, v]]
                z[r, g][:, v] = D[r, g, v] * (R[r, g][:, v] - s)
        ghosts(z, S)
    return {"y": z[..., :V].reshape(N, 128, V).astype(np.float32)}

from concourse.bass import DstId, RemoteDMATransfer
from concourse.mybir import AluOpType as A, AxisListType, ActivationFunctionType as F

V, GH, E, M, H, NR = 2048, 256, 6, 560, 80, 4
SL = M + 3 * H
KC = SL // 16
NS = 4 * SL
STAGES = 8
CHUNKS = [(35, 40), (40, 50), (0, 10), (10, 20), (20, 30), (30, 35)]
ACT_HALVES = 10

f32, bf, i32, u16 = "float32", "bfloat16", "int32", "uint16"
SCRATCH = {}
for _dt, _list in (
    (i32, dict(hal_i=48, hue_t=128, hueW=V, nb_i=768, pint=4, pand=4, tk=128, th=128, w1=128, w2=128, w8=48)),
    (u16, dict(hal_u=48, nb_u=768, au=128, ah=48, pu=200, xl=48, pq=200, yl=128, nl=4 * E * KC)),
    (bf, dict(permW=NS, pay=V, payH=768, coW=V, bW=V, onesb=768, ti=128, tr=128, wp=144, wq=144, wp2=144, wq2=144, sp=144, sq=144,
              bco=768, tmpb=128, bdi=128, ibf=128, mh=768, dp0=128, dp1=128, dp2=128, cs=NS, bs=NS)),
    (f32, dict(di_t=128, posW=V + 3 * GH, xW=V, ones=256, neg=128, pm=4, p800=4, p8=4, lt4=4, base3=4, hinit=4, cinit=4, cnt=4, oinit=4,
               tq=128, tmpm=128, tri=128, blk=128, s0=144, negi=128, mk=512, mk2=512, mk3=256, sown=128, sh=768, gp=768,
               w3=128, w4=128, w5=128, w6=128, w7=128, dr=128, dr2=128, xs=720, rm=E * V, t2=NS, dib=NS, zz=11 * SL,
               sa=480, sb=480, snd=7 * 240)),
):
    for _n in _list:
        SCRATCH[_n] = ("sbuf", [128, _list[_n]], _dt)
SCRATCH.update({"pf": ("sbuf", [128, 4, KC], f32), "xr": ("sbuf", [128, 3, 240], f32),
                "lf": ("sbuf", [128, E, 200], f32), "l1": ("sbuf", [128, E, KC], f32), "l2": ("sbuf", [128, E, KC], f32)})
for _k in range(8):
    SCRATCH["P%d" % _k] = ("psum", [128, 512], f32)
SEMAPHORES = ["cv", "ca", "cp", "cg", "loc", "rg", "rx"] + ["r%d" % _k for _k in range(7)] + ["d%d" % _k for _k in range(30)]


def rank_program(g, core, T, topo):
    rank = T.rank_of(core)
    if rank is None:
        return
    Q = {"v": g.vector, "a": g.scalar, "p": g.tensor, "g": g, "s": g.sync}
    count = {"cv": 0, "ca": 0, "cp": 0, "cg": 0, "loc": 0}
    waited = {q: {} for q in Q}
    lastw, readers, nd = {}, {}, [0]

    def wait(q, ev):
        if waited[q].get(ev[0], 0) < ev[1]:
            Q[q].wait_ge(T.sem[ev[0]], ev[1])
            waited[q][ev[0]] = ev[1]

    def deps(q, r, w):
        need = {}
        evs = [lastw[k] for k in list(r) + list(w) if k in lastw]
        for k in w:
            evs += readers.get(k, [])
        for k in r:
            if k[0] == "P":
                evs += [e for e in readers.get(k, []) if e[0] != "c" + q]
        for s, n in evs:
            if not (q == "p" and s == "cp"):
                need[s] = max(need.get(s, 0), n)
        for s in need:
            wait(q, (s, need[s]))

    def done(ev, r, w):
        for k in r:
            readers.setdefault(k, []).append(ev)
        for k in w:
            lastw[k] = ev
            readers[k] = []

    def op(q, r, w, *calls):
        deps(q, r, w)
        for c in calls:
            ins = c()
        s = "c" + q
        count[s] += 1
        ins.then_inc(T.sem[s], 1)
        done((s, count[s]), r, w)

    def dma(r, w, pairs, q="s"):
        deps(q, r, w)
        s = "d%d" % nd[0]
        nd[0] += 1
        for o, i in pairs:
            Q[q].dma_start(o, i).then_inc(T.sem[s], 16)
        count[s] = 16 * len(pairs)
        done((s, count[s]), r, w)

    peer = [T.cores[(rank + 3 - d) % NR] for d in range(3)]

    def send_one(r, d, out, src, sem):
        deps("g", r, [])
        rid, pid, _ = topo.addr(peer[d])
        g.remote_dma(out, src, T.sem[sem], T.sem.loc, pid, rid, topo.mask(core, peer[d]))
        count["loc"] += len(topo.engines(core, peer[d]))

    def send_two(r, items, sem):
        deps("g", r, [])
        trs = []
        for h, (d, out, src) in enumerate(items):
            es = topo.engines(core, peer[d])
            es = es[h * len(es) // 2:(h + 1) * len(es) // 2]
            rid, pid, _ = topo.addr(peer[d])
            trs.append(RemoteDMATransfer(dst_ids=[DstId(rid=rid, pnc=pid)], dma_engine_mask=sum(1 << e for e in es), remote_sem=T.sem[sem], src=src, dst=out))
            count["loc"] += len(es)
        g.remote_dma_fused(trs, local_sem=T.sem.loc)

    src_of = [T.cores[(rank + 1 + d) % NR] for d in range(3)]
    ARR = len(topo.engines(src_of[0], core)) + len(topo.engines(src_of[1], core)) // 2 + len(topo.engines(src_of[2], core)) // 2

    vec, act, pe = g.vector, g.scalar, g.tensor
    P = [T["P%d" % k] for k in range(8)]

    def ts(r, w, out, in0, s1, op0, s2=None, op1=None):
        if op1 is None:
            op("v", r, w, lambda: vec.tensor_scalar(out, in0, s1, None, op0))
        else:
            op("v", r, w, lambda: vec.tensor_scalar(out, in0, s1, s2, op0, op1))

    def tt(r, w, out, a, b, o):
        op("v", r, w, lambda: vec.tensor_tensor(out, a, b, o))

    def cp(q, r, w, out, in_):
        if q == "v":
            op("v", r, w, lambda: vec.tensor_copy(out, in_))
        else:
            op("a", r, w, lambda: act.activation(out, in_, F.Copy))

    def sel(r, w, out, in_, pat, cmp, base, cm):
        op("g", r, w, lambda: g.affine_select(out, in_, pat, cmp, 0.0, base, cm))

    def iota(w, out, pat, base, cm):
        op("g", [], w, lambda: g.iota(out, pat, base, cm, allow_small_or_imprecise_dtypes=True))

    def zero(key, buf, n):
        op("a", ["onesb"], [key], *[(lambda a=a: act.activation(buf[:, a:min(a + 768, n)], T.onesb[:, 0:min(768, n - a)], F.Copy, 0.0, 0.0)) for a in range(0, n, 768)])

    def to_list(r, bank, n, S, rhs_of):
        calls = [(lambda i=i: pe.matmul(P[bank][:, 0:n], T[S][:, 15 - i:143 - i], rhs_of(i), i == 0, i == 15)) for i in range(16)]
        op("p", list(r) + [S], ["P%d" % bank], *calls)

    def target(r, src, n, colour, ck, out, okey):
        cp("v", r, ["w1"], T.w1[:, 0:n], src)
        ts(r, ["w4"], T.w4[:, 0:n], src, 50.0, A.mult)
        ts([ck], ["w6"], T.w6[:, 0:n], colour, 750.0, A.mult)
        ts(["w1"], ["w2"], T.w2[:, 0:n], T.w1[:, 0:n], 4, A.logical_shift_right)
        tt(["w4", "w6"], ["w7"], T.w7[:, 0:n], T.w4[:, 0:n], T.w6[:, 0:n], A.add)
        ts(["w2"], ["w3"], T.w3[:, 0:n], T.w2[:, 0:n], -799.0, A.mult)
        tt(["w3", "w7"], ["w5"], T.w5[:, 0:n], T.w3[:, 0:n], T.w7[:, 0:n], A.add)
        cp("v", ["w5"], [okey], out, T.w5[:, 0:n])

    dma([], ["hal_i"], [(T.hal_i[:], T.halo[:])])
    dma([], ["hue_t"], [(T.hue_t[:], T.hue[:])])
    op("v", [], ["hueW"], lambda: vec.memset(T.hueW[:], 0))
    op("g", [], ["pint"], lambda: g.iota(T.pint[:, 0:1], [[0, 1]], 0, 1))
    op("g", [], ["tk"], lambda: g.iota(T.tk[:], [[1, 128]], 0, 0))
    iota(["base3"], T.base3[:, 0:3], [[-H, 3]], M + 2 * H - 1, 0)
    iota(["cinit"], T.cinit[:], [[SL, 4]], -1, 0)
    iota(["ti"], T.ti[:], [[0, 8], [1, 16]], 0, 0)
    iota(["tq"], T.tq[:], [[1, 8], [0, 16]], 0, 0)
    iota(["wp"], T.wp[:], [[16 * 127, 9], [0, 16]], 128 + 4 * 127, -127)
    iota(["wq"], T.wq[:], [[-16 * 15, 9], [0, 16]], 1 - 4 * 15, 15)
    ts(["pint"], ["pand"], T.pand[:, 0:1], T.pint[:, 0:1], 15, A.bitwise_and)
    op("v", [], ["ones"], lambda: vec.memset(T.ones[:], 1.0))
    cp("v", ["pand"], ["pm"], T.pm[:, 0:1], T.pand[:, 0:1])
    ts(["pand"], ["p800"], T.p800[:, 0:1], T.pand[:, 0:1], float(SL), A.mult)
    ts(["tk", "pm"], ["th"], T.th[:], T.tk[:], 0.0, A.mult, T.pm[:, 0:1], A.add)
    op("v", [], ["onesb"], lambda: vec.memset(T.onesb[:], 1.0))
    dma(["hueW", "tk"], ["hueA"], [(T.hueW[c::16, :], T.hue[:]) for c in range(4)] + [(T.hueW[5::16, :], T.tk[:])])
    dma(["hueW", "th"], ["hueB"], [(T.hueW[4::16, :], T.th[:])])
    dma([], ["nb_i"], [(T.nb_i[:, 128 * e:128 * e + 128], T.nb[:, V * e:V * e + V]) for e in range(E)])
    dma([], ["di_t"], [(T.di_t[:], T.di[:])])
    sel(["ones"], ["tmpm"], T.tmpm[:], T.ones[:, 0:128], [[-16, 8], [0, 16]], A.is_ge, 0, 1)
    sel(["tmpm"], ["tri"], T.tri[:], T.tmpm[:], [[1, 128]], A.is_gt, 0, -1)
    sel(["tmpm"], ["blk"], T.blk[:], T.tmpm[:], [[16, 8], [0, 16]], A.is_ge, 15, -1)
    sel(["ones"], ["s0"], T.s0[:], T.ones[:, 0:144], [[-16, 9], [200, 16]], A.is_equal, -3000, 1)
    for a, b, c in (("wp", "wp2", "sp"), ("wq", "wq2", "sq")):
        sel([a], [b], T[b][:], T[a][:], [[-16, 9], [200, 16]], A.is_ge, -3004, 1)
        sel([b], [c], T[c][:], T[b][:], [[16, 9], [0, 16]], A.is_ge, 5, -1)
    cp("v", ["hal_i"], ["hal_u"], T.hal_u[:], T.hal_i[:])
    ts(["pand"], ["lt4"], T.lt4[:, 0:1], T.pand[:, 0:1], 4.0, A.is_lt)
    ts(["pand"], ["p8"], T.p8[:, 0:1], T.pand[:, 0:1], 8.0, A.mult)
    for c in range(4):
        ts(["hue_t"], ["mk%d" % c], T.mk[:, 128 * c:128 * c + 128], T.hue_t[:], float(c), A.is_equal)
    ts(["base3", "p800"], ["hinit"], T.hinit[:, 0:3], T.base3[:, 0:3], T.p800[:, 0:1], A.add)
    ts(["tq", "p8"], ["tr"], T.tr[:], T.tq[:], T.p8[:, 0:1], A.add)
    for c in range(4):
        op("v", ["mk%d" % c], ["cnt%d" % c], lambda c=c: vec.tensor_reduce(T.cnt[:, c:c + 1], T.mk[:, 128 * c:128 * c + 128], AxisListType.X, A.add))
    op("p", ["tri"] + ["cnt%d" % c for c in range(4)], ["P5"], lambda: pe.matmul(P[5][:, 0:4], T.tri[:], T.cnt[:], True, True))
    zero("pay", T.pay, V)
    dma(["ti", "tr"], ["pay"], [(T.pay[4::16, :], T.ti[:]), (T.pay[5::16, :], T.tr[:])])
    zero("posO", T.posW, V)
    zero("permW", T.permW, NS)

    cp("v", ["hueA", "hueB", "hal_u"], ["payH"], T.payH[:], T.hueW[:].indirect(T.hal_u[:]))
    tt(["P5", "cinit"], ["oinit"], T.oinit[:], P[5][:, 0:4], T.cinit[:], A.add)
    ts(["payH", "pm", "lt4"], ["mh"], T.mh[:], T.payH[:], T.pm[:, 0:1], A.is_equal, T.lt4[:, 0:1], A.mult)
    hp = [P[0][:, 0:256], P[0][:, 256:512], P[1][:, 0:256]]
    for e in range(3):
        op("v", ["mh", "ones", "hinit"], ["P0" if e < 2 else "P1"],
           lambda e=e: vec.tensor_tensor_scan(hp[e], T.ones[:], T.mh[:, 256 * e:256 * e + 256], T.hinit[:, e:e + 1], A.mult, A.add))
    tt(["P0", "mh"], ["sh0"], T.sh[:, 0:512], P[0][:], T.mh[:, 0:512], A.mult)
    tt(["P1", "mh"], ["sh1"], T.sh[:, 512:768], P[1][:, 0:256], T.mh[:, 512:768], A.mult)
    op("p", ["blk", "sh0"], ["P2"], lambda: pe.matmul(P[2][:], T.blk[:], T.sh[:, 0:512], True, True))
    op("p", ["blk", "sh1"], ["P3"], lambda: pe.matmul(P[3][:, 0:256], T.blk[:], T.sh[:, 512:768], True, True))
    cp("a", ["P2"], ["gp0"], T.gp[:, 0:512], P[2][:])
    cp("a", ["P3"], ["gp1"], T.gp[:, 512:768], P[3][:, 0:256])
    send_two(["gp0"], [(d, T.posW[:, V + GH * d:V + GH * d + GH], T.gp[:, GH * (2 - d):GH * (3 - d)]) for d in (1, 2)], "rg")
    send_one(["gp1"], 0, T.posW[:, V:V + GH], T.gp[:, 512:768], "rg")
    lastw["posG"] = ("rg", ARR)
    to_list(["gp0", "gp1"], 6, 48, "s0", lambda i: T.gp[:, i::16])
    zero("coW", T.coW, V)

    for c in range(4):
        op("v", ["mk%d" % c, "ones", "oinit"], ["P4"],
           lambda c=c: vec.tensor_tensor_scan(P[4][:, 128 * c:128 * c + 128], T.ones[:, 0:128], T.mk[:, 128 * c:128 * c + 128], T.oinit[:, c:c + 1], A.mult, A.add))
    tt(["P4"] + ["mk%d" % c for c in range(4)], ["mk2"], T.mk2[:], P[4][:], T.mk[:], A.mult)
    tt(["mk2"], ["mk3"], T.mk3[:], T.mk2[:, 0:256], T.mk2[:, 256:512], A.add)
    tt(["mk3"], ["sown"], T.sown[:], T.mk3[:, 0:128], T.mk3[:, 128:256], A.add)
    dma(["sown"], ["posO"], [(T.posW[0::16, 0:V], T.sown[:])])
    dma([], ["coW"], [(T.coW[e::16, :], T.co[:, V * e:V * e + V]) for e in range(E)])
    dma(["posG"], ["xW"], [(T.xW[:], T.x[:])])
    dma([], ["bW"], [(T.bW[:], T.b[:])])
    cp("v", ["nb_i"], ["nb_u"], T.nb_u[:], T.nb_i[:])
    target(["sown"], T.sown[:], 128, T.hue_t[:], "hue_t", T.au[:], "au")
    op("v", [], ["neg"], lambda: vec.memset(T.neg[:], -1.0))
    cp("v", ["pay", "au"], ["permW"], T.permW[:].indirect(T.au[:]), T.pay[:])
    ts(["P6"], ["w3"], T.w3[:, 0:48], P[6][:, 0:48], 1.0 / SL, A.mult, -0.499, A.add)
    cp("v", ["w3"], ["w8"], T.w8[:], T.w3[:, 0:48])
    target(["P6"], P[6][:, 0:48], 48, T.w8[:], "w8", T.ah[:], "ah")
    cp("v", ["payH", "ah"], ["permW"], T.permW[:].indirect(T.ah[:]), T.payH[:])
    sel(["onesb"], ["bco"], T.bco[:], T.onesb[:], [[1, E], [16, 8], [0, 16]], A.is_equal, 0, -1)
    sel(["onesb"], ["tmpb"], T.tmpb[:], T.onesb[:, 0:128], [[-16, 8], [0, 16]], A.is_ge, -6, 1)
    sel(["tmpb"], ["bdi"], T.bdi[:], T.tmpb[:], [[16, 8], [0, 16]], A.is_ge, 8, -1)
    sel(["onesb"], ["ibf"], T.ibf[:], T.onesb[:, 0:128], [[-1, 128]], A.is_equal, 0, 1)
    sel(["neg"], ["negi"], T.negi[:], T.neg[:], [[-1, 128]], A.is_equal, 0, 1)
    to_list(["posO"], 7, 128, "s0", lambda i: T.posW[:, i:V:16])
    op("p", ["permW", "sp"], ["P4"],
       *[(lambda c=c, i=i: pe.matmul(P[4][:, KC * c:KC * c + KC], T.sp[:, 15 - i:143 - i], T.permW[:, SL * c + KC * i:SL * c + KC * i + KC], i == 0, i == 15))
         for c in range(4) for i in range(16)])
    to_list(["permW"], 5, 200, "sq", lambda i: T.permW[:, i::16])

    def remap(q, h):
        cp(q, ["posO", "posG", "nb_u"], ["rm%d" % h], T.rm[:, 1024 * h:1024 * h + 1024], T.posW[:].indirect(T.nb_u[:, 64 * h:64 * h + 64]))

    def row_up(e):
        dma(["rm%d" % (2 * e), "rm%d" % (2 * e + 1), "rm0", "rm1"], ["t1_%d" % e], [(T.rm[e::16, 0:V], T.rm[0::16, V * e:V * e + V])])

    cp("v", ["di_t"], ["dp0"], T.dp0[:], T.di_t[:])
    cp("v", ["P7"], ["yl"], T.yl[:], P[7][:, 0:128])
    tt(["di_t", "dp0"], ["dr"], T.dr[:], T.di_t[:], T.dp0[:], A.subtract)
    cp("v", ["dr"], ["dp1"], T.dp1[:], T.dr[:])
    tt(["dr", "dp1"], ["dr2"], T.dr2[:], T.dr[:], T.dp1[:], A.subtract)
    cp("v", ["dr2"], ["dp2"], T.dp2[:], T.dr2[:])
    dma(["dp0", "dp1", "dp2", "coW"], ["coD"], [(T.coW[6 + k::16, :], T["dp%d" % k][:]) for k in range(3)])
    remap("v", 11)
    cp("v", ["P4"], ["pf"], T.pf[:], P[4][:, 0:200])
    cp("v", ["P4"], ["pu"], T.pu[:], P[4][:, 0:200])
    for d in range(3):
        cp("v", ["pf"], ["xl%d" % d], T.xl[:, 15 * d:15 * d + 15], T.pf[:, 1:4, 35 + 5 * d:40 + 5 * d])
    cp("v", ["xW", "xl0", "xl1", "xl2"], ["xs"], T.xs[:], T.xW[:].indirect(T.xl[:, 0:45]))
    cp("v", ["P5"], ["pq"], T.pq[:], P[5][:, 0:200])
    send_two(["xs"], [(d, T.xr[:, d, :], T.xs[:, 240 * d:240 * d + 240]) for d in (1, 2)], "rx")
    send_one(["xs"], 0, T.xr[:, 0, :], T.xs[:, 0:240], "rx")
    lastw["xr"] = ("rx", ARR)
    for h in range(ACT_HALVES):
        remap("a", h)
    for h in range(10, ACT_HALVES - 1, -1):
        remap("v", h)
    for e in (1, 2, 3, 5, 4):
        row_up(e)

    def sort_co(q, c):
        cp(q, ["coW", "coD", "pu"], ["cs%d" % c], T.cs[:, SL * c:SL * c + SL], T.coW[:].indirect(T.pu[:, KC * c:KC * c + KC]))

    def sort_b(q, c):
        cp(q, ["bW", "pu"], ["bs%d" % c], T.bs[:, SL * c:SL * c + SL], T.bW[:].indirect(T.pu[:, KC * c:KC * c + KC]))

    def sort_x(q, c):
        cp(q, ["xW", "pu"], ["zo%d" % (c - 1)], T.zz[:, SL * (c - 1):SL * (c - 1) + M], T.xW[:].indirect(T.pu[:, KC * c:KC * c + 35]))

    def sort_nb(q, key, a, b):
        cp(q, ["rm0", "rm1", "pq"] + ["t1_%d" % e for e in range(1, E)], [key], T.t2[:, 16 * a:16 * b], T.rm[:, 0:V].indirect(T.pq[:, a:b]))

    def nb_lists(c, keys):
        dma(keys, ["lf%d" % c], [(T.lf[:, e, KC * c:KC * c + KC], T.t2[e::16, SL * c:SL * c + SL]) for e in range(E)])

    def di_mm(c):
        for h in range(2):
            op("p", ["bdi", "cs%d" % c], ["P%d" % (6 + h)],
               lambda h=h: pe.matmul(P[6 + h][:, 0:400], T.bdi[:], T.cs[:, SL * c + 400 * h:SL * c + 400 * h + 400], True, True))

    def di_cp(c):
        for h in range(2):
            cp("a", ["P%d" % (6 + h)], ["dib%d" % c], T.dib[:, SL * c + 400 * h:SL * c + 400 * h + 400], P[6 + h][:, 0:400])

    sort_x("v", 1)
    sort_x("v", 2)
    sort_co("a", 0)
    di_mm(0)
    sort_x("a", 3)
    sort_nb("a", "t2a", 0, 26)
    sort_nb("v", "t2b", 26, KC)
    nb_lists(0, ["t2a", "t2b"])
    sort_nb("v", "t2c", KC, 3 * KC)
    sort_nb("v", "t2d", 3 * KC, 4 * KC)
    nb_lists(1, ["t2c"])
    sort_b("a", 0)
    di_cp(0)
    for c in range(3):
        cp("a", ["xr"], ["zg%d" % c], T.zz[:, SL * c + M:SL * c + SL], T.xr[:, :, H * c:H * c + H])

    def lcol(c, k):
        return E * KC * c + E * sum(b - a for a, b in CHUNKS[:k])

    def lists(c):
        q, lk = T.lf[:, :, KC * c:KC * c + KC], "lf%d" % c
        if c in (1, 2):
            ts([lk], ["l1"], T.l1[:], q, float(SL * c), A.is_lt, float(NS), A.mult)
            tt([lk, "l1"], ["l2"], T.l2[:], q, T.l1[:], A.add)
        for k, (a, b) in enumerate(CHUNKS):
            out = T.nl[:, lcol(c, k):lcol(c, k) + E * (b - a)]
            if c == 3:
                ts([lk], ["nl%d_%d" % (c, k)], out, T.lf[:, :, KC * c + a:KC * c + b], float(3 * SL - 1), A.min)
            elif c == 0:
                ts([lk], ["nl%d_%d" % (c, k)], out, T.lf[:, :, a:b], -float(SL), A.add, 0.0, A.max)
            else:
                ts(["l2"], ["nl%d_%d" % (c, k)], out, T.l2[:, :, a:b], -float(SL * (c + 1)), A.add, 0.0, A.max)

    lists(0)

    turn = [0]
    for s in range(STAGES):
        c = s % 4
        ks = list(range(len(CHUNKS))) if s < STAGES - 1 else [5, 2, 3, 4]
        win = T.zz[:, SL * s:SL * s + 3 * SL]
        wk = ["zo%d" % n for n in (s, s + 1, s + 2)] + ["zg%d" % n for n in (s, s + 1, s + 2)]
        info = []
        for j, k in enumerate(ks):
            a, b = CHUNKS[k]
            n, g0, l0, w = 16 * (b - a), V + 16 * lcol(0, k), lcol(c, k), b - a
            info.append((k, a, b, n, g0, SL * c + 16 * a, (turn[0] + j) % 2))
            rk = wk + ["nl%d_%d" % (c, k)]
            if j == 1 and s not in (1, 2):
                cp("v", rk, ["gb%db" % k], T.rm[:, g0 + 3 * n:g0 + E * n], win.indirect(T.nl[:, l0 + 3 * w:l0 + E * w]))
                cp("a", rk, ["gb%da" % k], T.rm[:, g0:g0 + 3 * n], win.indirect(T.nl[:, l0:l0 + 3 * w]))
            else:
                cp("a", rk, ["gb%da" % k, "gb%db" % k], T.rm[:, g0:g0 + E * n], win.indirect(T.nl[:, l0:l0 + E * w]))
        turn[0] += len(info)
        if s < 3:
            sort_co("a", c + 1)
            sort_b("a", c + 1)
            if s > 0:
                lists(c + 1)

        def bcast(j):
            k, a, b, n, g0, c0, u = info[j]
            for h in range(2):
                op("p", ["bco", "cs%d" % c], ["P%d" % (3 * u + h)],
                   *[(lambda e=e: pe.matmul(P[3 * u + h][:, n * e:n * e + n], T.bco[:, 128 * (3 * h + e):128 * (3 * h + e) + 128], T.cs[:, c0:c0 + n], True, True)) for e in range(3)])

        def final(j):
            k, a, b, n, g0, c0, u = info[j]
            if a >= 35:
                o0 = 240 * s + 16 * (a - 35)
                tt(["P%d" % (3 * u + 2), "dib%d" % c], ["snd%d" % k], T.snd[:, o0:o0 + n], P[3 * u + 2][:, 0:n], T.dib[:, c0:c0 + n], A.mult)
                z0 = SL * (3 + s) + M
                if k == 0:
                    send_one(["snd0"], 0, T.zz[:, z0:z0 + H], T.snd[:, o0:o0 + H], "r%d" % s)
                else:
                    send_two(["snd1"], [(d, T.zz[:, z0 + H * d:z0 + H * d + H], T.snd[:, 240 * s + H * d:240 * s + H * d + H]) for d in (1, 2)], "r%d" % s)
                    lastw["zg%d" % (3 + s)] = ("r%d" % s, ARR)
                    if s < 2:
                        nb_lists(s + 2, ["t2c", "t2d", "snd1"])
            else:
                z0 = SL * (3 + s) + 16 * a
                tt(["P%d" % (3 * u + 2), "dib%d" % c], ["zo%d" % (3 + s)], T.zz[:, z0:z0 + n], P[3 * u + 2][:, 0:n], T.dib[:, c0:c0 + n], A.mult)

        bcast(0)
        bcast(1)
        for j in range(len(info)):
            k, a, b, n, g0, c0, u = info[j]
            S, sk, pa, pb, pc = (T.sa, T.sb)[u], "sum%d" % u, "P%d" % (3 * u), "P%d" % (3 * u + 1), "P%d" % (3 * u + 2)
            tt(["gb%da" % k, pa], [pa], P[3 * u][:, 0:3 * n], T.rm[:, g0:g0 + 3 * n], P[3 * u][:, 0:3 * n], A.mult)
            tt(["gb%db" % k, pb], [sk], S[:, 0:3 * n], T.rm[:, g0 + 3 * n:g0 + 6 * n], P[3 * u + 1][:, 0:3 * n], A.mult)
            tt([pa, sk], [sk], S[:, 0:3 * n], S[:, 0:3 * n], P[3 * u][:, 0:3 * n], A.add)
            if s < 3 and j == len(info) - 1:
                di_mm(c + 1)
            op("p", ["ibf", "bs%d" % c], [pc], lambda: pe.matmul(P[3 * u + 2][:, 0:n], T.ibf[:], T.bs[:, c0:c0 + n], True, False))
            op("p", ["negi", sk], [pc], *[(lambda e=e: pe.matmul(P[3 * u + 2][:, 0:n], T.negi[:], S[:, n * e:n * e + n], False, e == 2)) for e in range(3)])
            if j + 2 < len(info):
                bcast(j + 2)
            if j > 0:
                final(j - 1)
        if s == 0:
            lists(1)
        final(len(info) - 1)
        if s < 3:
            di_cp(c + 1)

    win = T.zz[:, 7 * SL:10 * SL + M]
    wk = ["zo%d" % n for n in range(7, 11)] + ["zg%d" % n for n in range(7, 10)] + ["yl"]
    for h, q in ((0, "a"), (2, "v"), (1, "a"), (3, "v")):
        yo = T.rm[:, 4 * V + 512 * h:4 * V + 512 * h + 512]
        cp(q, wk, ["yo%d" % h], yo, win.indirect(T.yl[:, 32 * h:32 * h + 32]))
        dma(["yo%d" % h], [], [(T.y[:, 512 * h:512 * h + 512], yo)])
    for s in count:
        wait("g", (s, count[s]))
